import numpy as np
import ml_dtypes


def mxq(x, axis, fmt="e4m3"):
    dtype, down = {"e4m3": (ml_dtypes.float8_e4m3fn, 7), "e5m2": (ml_dtypes.float8_e5m2, 14)}[fmt]
    v = np.moveaxis(np.asarray(x, np.float32).astype(ml_dtypes.bfloat16).astype(np.float64), axis, -1)
    blocks = v.reshape(v.shape[:-1] + (-1, 32))
    amax = np.abs(blocks).max(-1, keepdims=True)
    byte = np.maximum(np.where(amax > 0, np.frexp(amax)[1] - 1 + 127, 0) - down, 1)
    scale = np.exp2(byte - 127.0)
    codes = (blocks / scale).astype(np.float32).astype(dtype).astype(np.float64)
    return np.moveaxis((codes * scale).reshape(v.shape), -1, axis)


WIDE = False


def mx_kscale(k):
    if not WIDE:
        return np.ones(k)
    levels = np.array([10, -10, 5, -5, 0])
    if k % 512:
        return np.exp2(np.random.permutation(np.resize(levels, k // 32))).repeat(32)
    a = np.empty((k // 512, 16))
    for p in range(k // 512):
        a[p, :8] = np.random.permutation(np.resize(levels, 8))
        for g in range(8):
            far = levels[np.abs(levels - a[p, g]) >= 10]
            a[p, g + 8] = far[np.random.randint(len(far))]
    return np.exp2(a.ravel()).repeat(32)


def f64(x):
    return np.asarray(x).astype(np.float64)


def striped(idx):
    return np.tile(np.asarray(idx).reshape(-1, 16).T, (8, 1)).astype(np.uint16)


def unstriped(offs):
    return offs[:16].T.reshape(-1).astype(np.int64)


E2M1 = np.array([0.0, 0.5, 1.0, 1.5, 2.0, 3.0, 4.0, 6.0, -0.0, -0.5, -1.0, -1.5, -2.0, -3.0, -4.0, -6.0])


def pack_weight(w, fmt):
    k, n = w.shape
    w = f64(np.asarray(w, np.float32).astype(ml_dtypes.bfloat16)).reshape(k // 32, 32, n)
    amax = np.abs(w).max(1)
    if fmt == "e4m3":
        byte = np.frexp(amax)[1] - 1 + 127 - 7
    else:
        mant, ex = np.frexp(amax / 6.0)
        byte = np.where(mant > 0.5, ex, ex - 1) + 127
    byte = np.clip(np.where(amax > 0, byte, 1), 1, 254)
    scaled = (w * np.exp2(127.0 - byte)[:, None, :]).reshape(k, n).astype(np.float32)
    by_word = np.ascontiguousarray(scaled.reshape(k // 512, 128, 4, n).transpose(0, 1, 3, 2))
    if fmt == "e4m3":
        words = by_word.astype(ml_dtypes.float8_e4m3fn).view(np.uint8)
    else:
        c = by_word.astype(ml_dtypes.float4_e2m1fn).view(np.uint8) & 0xF
        words = (c[..., 0::2] | (c[..., 1::2] << 4)).reshape(k // 512, 128, 2 * n)
    return np.ascontiguousarray(words), np.ascontiguousarray(byte.astype(np.uint8).reshape(k // 512, 16, n))


def unpack_weight(words, scales, fmt):
    g, _, n = scales.shape
    words = np.ascontiguousarray(words).reshape(g, 128, n, -1)
    if fmt == "e4m3":
        vals = words.view(ml_dtypes.float8_e4m3fn).astype(np.float64)
    else:
        nib = np.empty((g, 128, n, 4), np.uint8)
        nib[..., 0::2] = words & 0xF
        nib[..., 1::2] = words >> 4
        vals = E2M1[nib]
    vals = vals * np.repeat(np.exp2(scales.astype(np.float64) - 127.0), 8, axis=1)[..., None]
    return vals.transpose(0, 1, 3, 2).reshape(g * 512, n)


K, T, J, B, L, N = 1024, 2048, 512, 128, 512, 512


def setup_inputs():
    n = np.random.standard_normal
    idx = np.random.permutation(T)[:J]
    fk = mx_kscale(K)
    fl = mx_kscale(L)
    xtp = pack_weight(n((K, T)) / fk[:, None], "e4m3")
    wp = pack_weight(n((K, N)) * 1 / np.sqrt(K) * fk[:, None], "e2m1")
    wsp = pack_weight(n((L, N)) * 1 / np.sqrt(L) * fl[:, None], "e4m3")
    return {
        "xt_words": xtp[0],
        "xt_scales": xtp[1],
        "w_words": wp[0],
        "w_scales": wp[1],
        "xs": (n((L, J)) / fl[:, None]).astype(np.float32),
        "ws_words": wsp[0],
        "ws_scales": wsp[1],
        "offs": striped(idx),
    }


def reference(xt_words, xt_scales, w_words, w_scales, xs, ws_words, ws_scales, offs):
    idx = unstriped(offs)
    xtu = unpack_weight(xt_words, xt_scales, "e4m3")
    wu = unpack_weight(w_words, w_scales, "e2m1")
    wsu = unpack_weight(ws_words, ws_scales, "e4m3")
    xtidxg = xtu[:, idx]
    z = wu.T @ xtidxg
    u = z.reshape(N, B, J // B).max(axis=2)
    ur = np.repeat(u, J // B, axis=1)
    xsq = mxq(f64(xs), 0, "e4m3")
    q = wsu.T @ xsq
    y = z * np.exp(z - ur) + 0.5 * q
    return y

@@ -1,0 +1,189 @@
+from contextlib import ExitStack
+
+import concourse.mybir as mybir
+
+K, T, J, L, N = 1024, 2048, 512, 512, 512
+FLOPS = 2 * N * J * (K + L)
+
+F32 = mybir.dt.float32
+BF16 = mybir.dt.bfloat16
+I32 = mybir.dt.int32
+U32 = mybir.dt.uint32
+U16 = mybir.dt.uint16
+U8 = mybir.dt.uint8
+FP8X4 = mybir.dt.float8_e4m3fn_x4
+FP4X4 = mybir.dt.float4_e2m1fn_x4
+ALU = mybir.AluOpType
+ACT = mybir.ActivationFunctionType
+
+P = 128
+PACK = 4
+PASSES = K // (P * PACK)
+GROUP = 4
+HALF = J // 2
+PAIRS = N // (2 * P)
+
+
+def load_scale_rows(queue, plane, rows):
+    passes = rows.shape[0]
+    src = rows.bitcast(I32).rearrange("z (q r) c -> r q z c", r=4)
+    dst = plane[:].bitcast(I32)
+    for r in range(4):
+        queue.dma_start(out=dst[r:P:32, :].rearrange("q (z c) -> q z c", z=passes), in_=src[r])
+
+
+def tile_list_peak_gated_members_kernel(tc, xt_words, xt_scales, w_words, w_scales, xs, ws_words, ws_scales, offs, out):
+    nc = tc.nc
+    with ExitStack() as ctx:
+        keep = ctx.enter_context(tc.tile_pool(name="keep", bufs=1))
+        psum = ctx.enter_context(tc.psum_pool(name="psum", bufs=1))
+
+        offsets = keep.tile([P, J // 16], U16, name="offsets")
+        xt = [keep.tile([P, T], U32, name="xt%d" % z, align_bytes=64) for z in range(PASSES)]
+        xt_sc = keep.tile([P, PASSES * T], U8, name="xt_sc", align_bytes=64)
+        w = [keep.tile([P, 2 * N], U8, name="w%d" % z, align_bytes=64) for z in range(PASSES)]
+        w_sc = keep.tile([P, PASSES * N], U8, name="w_sc", align_bytes=64)
+        ws = keep.tile([P, N], U32, name="ws", align_bytes=64)
+        ws_sc = keep.tile([P, N], U8, name="ws_sc", align_bytes=64)
+        xs_raw = [keep.tile([P, PACK, HALF], F32, name="xs_raw%d" % h) for h in range(2)]
+
+        nc.vector.memset(xt_sc[:].bitcast(I32), 0)
+        nc.vector.memset(w_sc[:].bitcast(I32), 0)
+        nc.vector.memset(ws_sc[:].bitcast(I32), 0)
+
+        def load_words(z):
+            nc.sync.dma_start(out=xt[z][:].bitcast(I32), in_=xt_words[z].rearrange("p c r -> p (c r)").bitcast(I32))
+
+        def load_xs(h):
+            nc.sync.dma_start(out=xs_raw[h][:], in_=xs.rearrange("(p i) j -> p i j", i=PACK)[:, :, h * HALF : (h + 1) * HALF])
+
+        def load_w(z):
+            nc.sync.dma_start(out=w[z][:].bitcast(I32), in_=w_words[z].bitcast(I32))
+
+        nc.sync.dma_start(offsets[:], offs)
+        load_words(0)
+        load_scale_rows(nc.sync, xt_sc, xt_scales)
+        load_words(1)
+        load_w(0)
+        load_scale_rows(nc.sync, w_sc, w_scales)
+        load_w(1)
+        load_xs(0)
+        nc.sync.dma_start(out=ws[:].bitcast(I32), in_=ws_words[0].rearrange("p c r -> p (c r)").bitcast(I32))
+        load_scale_rows(nc.sync, ws_sc, ws_scales)
+        load_xs(1)
+
+        picked0 = keep.tile([P, J], U32, name="picked0", align_bytes=64)
+        picked1 = [keep.tile([P, HALF], U32, name="picked1_%d" % h, align_bytes=64) for h in range(2)]
+        picked_sc = [keep.tile([P, J], U8, name="picked_sc%d" % z, align_bytes=64) for z in range(PASSES)]
+        nc.vector.tensor_copy(picked0[:], xt[0][:].indirect(offsets[:]))
+        for z in range(PASSES):
+            nc.vector.tensor_copy(picked_sc[z][:], xt_sc[:, z * T : (z + 1) * T].indirect(offsets[:]))
+        for h in range(2):
+            nc.vector.tensor_copy(picked1[h][:], xt[1][:].indirect(offsets[:, h * HALF // 16 : (h + 1) * HALF // 16]))
+
+        units = [(h, pair) for h in range(2) for pair in range(PAIRS)]
+        zb = [psum.tile([P, 2 * HALF], F32, name="z%d" % u) for u in range(len(units))]
+        qb = [psum.tile([P, 2 * HALF], F32, name="q%d" % u) for u in range(len(units))]
+
+        def z_pass(u, z):
+            h, pair = units[u]
+            cols = slice(h * HALF, (h + 1) * HALF)
+            moving = picked0[:, cols] if z == 0 else picked1[h][:]
+            for a in range(2):
+                t = 2 * pair + a
+                nc.tensor.matmul_mx(
+                    out=zb[u][:, a * HALF : (a + 1) * HALF],
+                    lhsT=w[z][:, 2 * P * t : 2 * P * (t + 1)].bitcast(FP4X4),
+                    lhsT_scale=w_sc[:, z * N + P * t : z * N + P * (t + 1)],
+                    rhs=moving.bitcast(FP8X4),
+                    rhs_scale=picked_sc[z][:, cols],
+                    start=(z == 0 and a == 0),
+                    stop=(z == PASSES - 1 and a == 1),
+                )
+
+        for u in range(len(units)):
+            for z in range(PASSES):
+                z_pass(u, z)
+
+        xs_bf = [keep.tile([P, HALF, PACK], BF16, name="xs_bf%d" % h, align_bytes=64) for h in range(2)]
+        xq = [keep.tile([P, HALF], U32, name="xq%d" % h, align_bytes=64) for h in range(2)]
+        xq_sc = [keep.tile([P, HALF], U8, name="xq_sc%d" % h, align_bytes=64) for h in range(2)]
+
+        def round_xs(h):
+            nc.scalar.activation(
+                out=xs_bf[h][:].rearrange("p (c i) t -> p c t i", i=4),
+                in_=xs_raw[h][:].rearrange("p t (c i) -> p c t i", i=4),
+                func=ACT.Copy,
+            )
+
+        def q_product(h):
+            nc.vector.quantize_mx(out=xq[h][:].bitcast(FP8X4), scales=xq_sc[h][:], in_=xs_bf[h][:].rearrange("p c t -> p (c t)"))
+            for pair in range(PAIRS):
+                for a in range(2):
+                    t = 2 * pair + a
+                    nc.tensor.matmul_mx(
+                        out=qb[h * PAIRS + pair][:, a * HALF : (a + 1) * HALF],
+                        lhsT=ws[:, P * t : P * (t + 1)].bitcast(FP8X4),
+                        lhsT_scale=ws_sc[:, P * t : P * (t + 1)],
+                        rhs=xq[h][:].bitcast(FP8X4),
+                        rhs_scale=xq_sc[h][:],
+                        start=True,
+                        stop=True,
+                    )
+
+        W = 2 * HALF
+        peak = [keep.tile([P, W // GROUP], F32, name="peak%d" % u) for u in range(len(units))]
+        gap = [keep.tile([P, W], F32, name="gap%d" % u) for u in range(len(units))]
+        gate = [keep.tile([P, W], F32, name="gate%d" % u) for u in range(len(units))]
+        kept = [keep.tile([P, W], F32, name="kept%d" % u) for u in range(len(units))]
+        half_q = [keep.tile([P, W], F32, name="half_q%d" % u) for u in range(len(units) - 1)]
+        res = [keep.tile([P, W], F32, name="res%d" % u) for u in range(len(units))]
+        out_v = out.rearrange("(t p) j -> p t j", p=P)
+
+        def find_peak(u):
+            nc.vector.tensor_reduce(out=peak[u][:], in_=zb[u][:].rearrange("p (g m) -> p g m", m=GROUP), axis=mybir.AxisListType.X, op=ALU.max)
+
+        def find_gate(u):
+            nc.vector.tensor_tensor(
+                out=gap[u][:].rearrange("p (g m) -> p g m", m=GROUP),
+                in0=zb[u][:].rearrange("p (g m) -> p g m", m=GROUP),
+                in1=peak[u][:].unsqueeze(2).to_broadcast([P, W // GROUP, GROUP]),
+                op=ALU.subtract,
+            )
+            nc.scalar.activation(out=gate[u][:], in_=gap[u][:], func=ACT.Exp)
+
+        def apply_gate(u):
+            nc.vector.tensor_tensor(out=kept[u][:], in0=zb[u][:], in1=gate[u][:], op=ALU.mult)
+
+        def finish(u):
+            h, pair = units[u]
+            if u < len(units) - 1:
+                nc.scalar.activation(out=half_q[u][:], in_=qb[u][:], func=ACT.Copy, scale=0.5)
+                nc.gpsimd.tensor_tensor(out=res[u][:], in0=kept[u][:], in1=half_q[u][:], op=ALU.add)
+            else:
+                nc.vector.scalar_tensor_tensor(out=res[u][:], in0=qb[u][:], scalar=0.5, in1=kept[u][:], op0=ALU.mult, op1=ALU.add)
+            nc.sync.dma_start(
+                out=out_v[:, 2 * pair : 2 * pair + 2, h * HALF : (h + 1) * HALF],
+                in_=res[u][:].rearrange("p (a c) -> p a c", a=2),
+            )
+
+        round_xs(0)
+        find_peak(0)
+        find_peak(1)
+        find_gate(0)
+        q_product(0)
+        find_gate(1)
+        find_peak(2)
+        apply_gate(0)
+        finish(0)
+        round_xs(1)
+        find_gate(2)
+        apply_gate(1)
+        finish(1)
+        find_peak(3)
+        q_product(1)
+        find_gate(3)
+        apply_gate(2)
+        finish(2)
+        apply_gate(3)
+        finish(3)

@@ -36,74 +36,84 @@ def tile_list_peak_gated_members_kernel(tc, xt_words, xt_scales, w_words, w_scal
     nc = tc.nc
     with ExitStack() as ctx:
         keep = ctx.enter_context(tc.tile_pool(name="keep", bufs=1))
+        shared = ctx.enter_context(tc.tile_pool(name="shared", bufs=1))
         psum = ctx.enter_context(tc.psum_pool(name="psum", bufs=1))
 
         offsets = keep.tile([P, J // 16], U16, name="offsets")
-        xt = [keep.tile([P, T], U32, name="xt%d" % z, align_bytes=64) for z in range(PASSES)]
-        xt_sc = keep.tile([P, PASSES * T], U8, name="xt_sc", align_bytes=64)
-        w = [keep.tile([P, 2 * N], U8, name="w%d" % z, align_bytes=64) for z in range(PASSES)]
+        xt = [keep.tile([P, T], U32, name="xt%d" % z, tag="xt_slot%d" % z, align_bytes=64) for z in range(PASSES)]
+        xt_sc = shared.tile([P, T], U8, name="xt_sc", align_bytes=64, offset=4032)
+        w = keep.tile([P, PASSES, 2 * N], U8, name="w", align_bytes=64)
         w_sc = keep.tile([P, PASSES * N], U8, name="w_sc", align_bytes=64)
-        ws = keep.tile([P, N], U32, name="ws", align_bytes=64)
-        ws_sc = keep.tile([P, N], U8, name="ws_sc", align_bytes=64)
-        xs_raw = [keep.tile([P, PACK, HALF], F32, name="xs_raw%d" % h) for h in range(2)]
+        ws = keep.tile([P, N], U32, name="ws", tag="xt_slot0", align_bytes=64)
+        ws_sc = shared.tile([P, N], U8, name="ws_sc", align_bytes=64, offset=4096)
+        xs_raw = [
+            shared.tile([P, PACK, HALF], F32, name="xs_raw0", align_bytes=64, offset=0),
+            shared.tile([P, PACK, HALF], F32, name="xs_raw1", align_bytes=64, offset=6016),
+        ]
+        moved_sc = keep.tile([P, J], U8, name="moved_sc", align_bytes=64)
 
         nc.vector.memset(xt_sc[:].bitcast(I32), 0)
-        nc.vector.memset(w_sc[:].bitcast(I32), 0)
-        nc.vector.memset(ws_sc[:].bitcast(I32), 0)
+        nc.gpsimd.memset(w_sc[:].bitcast(I32), 0)
+        nc.gpsimd.memset(moved_sc[:].bitcast(I32), 0)
 
-        def load_words(z):
-            nc.sync.dma_start(out=xt[z][:].bitcast(I32), in_=xt_words[z].rearrange("p c r -> p (c r)").bitcast(I32))
+        def load_words(z, cols):
+            nc.sync.dma_start(out=xt[z][:].bitcast(I32)[:, cols], in_=xt_words[z].rearrange("p c r -> p (c r)").bitcast(I32)[:, cols])
 
         def load_xs(h):
             nc.sync.dma_start(out=xs_raw[h][:], in_=xs.rearrange("(p i) j -> p i j", i=PACK)[:, :, h * HALF : (h + 1) * HALF])
 
-        def load_w(z):
-            nc.sync.dma_start(out=w[z][:].bitcast(I32), in_=w_words[z].bitcast(I32))
-
         nc.sync.dma_start(offsets[:], offs)
-        load_words(0)
-        load_scale_rows(nc.sync, xt_sc, xt_scales)
-        load_words(1)
-        load_w(0)
+        load_words(0, slice(0, T // 2))
+        for r in range(4):
+            nc.sync.dma_start(
+                out=xt_sc[:].bitcast(I32)[r:P:16, :],
+                in_=xt_scales.bitcast(I32).rearrange("z (q r) c -> r q z c", r=4)[r],
+            )
+        load_words(0, slice(T // 2, T))
+        nc.sync.dma_start(out=w[:].bitcast(I32), in_=w_words.bitcast(I32).rearrange("z p c -> p z c"))
         load_scale_rows(nc.sync, w_sc, w_scales)
-        load_w(1)
-        load_xs(0)
-        nc.sync.dma_start(out=ws[:].bitcast(I32), in_=ws_words[0].rearrange("p c r -> p (c r)").bitcast(I32))
-        load_scale_rows(nc.sync, ws_sc, ws_scales)
-        load_xs(1)
+        load_words(1, slice(0, T))
 
-        picked0 = keep.tile([P, J], U32, name="picked0", align_bytes=64)
-        picked1 = [keep.tile([P, HALF], U32, name="picked1_%d" % h, align_bytes=64) for h in range(2)]
-        picked_sc = [keep.tile([P, J], U8, name="picked_sc%d" % z, align_bytes=64) for z in range(PASSES)]
-        nc.vector.tensor_copy(picked0[:], xt[0][:].indirect(offsets[:]))
+        picked = [[keep.tile([P, HALF], U32, name="picked%d_%d" % (z, h), align_bytes=64) for h in range(2)] for z in range(PASSES)]
+        both_sc = keep.tile([P, J], U8, name="both_sc", align_bytes=64)
+        picked_sc = [both_sc, moved_sc]
+        nc.vector.tensor_copy(both_sc[:], xt_sc[:].indirect(offsets[:]))
+        nc.sync.dma_start(out=moved_sc[:].bitcast(I32)[0 : P - 16, :], in_=both_sc[:].bitcast(I32)[16:P, :])
+        load_xs(0)
+        load_xs(1)
+        nc.gpsimd.memset(ws_sc[:].bitcast(I32), 0)
+        load_scale_rows(nc.sync, ws_sc, ws_scales)
         for z in range(PASSES):
-            nc.vector.tensor_copy(picked_sc[z][:], xt_sc[:, z * T : (z + 1) * T].indirect(offsets[:]))
-        for h in range(2):
-            nc.vector.tensor_copy(picked1[h][:], xt[1][:].indirect(offsets[:, h * HALF // 16 : (h + 1) * HALF // 16]))
+            for h in range(2):
+                nc.vector.tensor_copy(picked[z][h][:], xt[z][:].indirect(offsets[:, h * HALF // 16 : (h + 1) * HALF // 16]))
+        nc.sync.dma_start(out=ws[:].bitcast(I32), in_=ws_words[0].rearrange("p c r -> p (c r)").bitcast(I32))
 
         units = [(h, pair) for h in range(2) for pair in range(PAIRS)]
         zb = [psum.tile([P, 2 * HALF], F32, name="z%d" % u) for u in range(len(units))]
         qb = [psum.tile([P, 2 * HALF], F32, name="q%d" % u) for u in range(len(units))]
 
-        def z_pass(u, z):
+        def z_pass(u, z, opens):
             h, pair = units[u]
             cols = slice(h * HALF, (h + 1) * HALF)
-            moving = picked0[:, cols] if z == 0 else picked1[h][:]
             for a in range(2):
                 t = 2 * pair + a
                 nc.tensor.matmul_mx(
                     out=zb[u][:, a * HALF : (a + 1) * HALF],
-                    lhsT=w[z][:, 2 * P * t : 2 * P * (t + 1)].bitcast(FP4X4),
+                    lhsT=w[:, z, 2 * P * t : 2 * P * (t + 1)].bitcast(FP4X4),
                     lhsT_scale=w_sc[:, z * N + P * t : z * N + P * (t + 1)],
-                    rhs=moving.bitcast(FP8X4),
+                    rhs=picked[z][h][:].bitcast(FP8X4),
                     rhs_scale=picked_sc[z][:, cols],
-                    start=(z == 0 and a == 0),
-                    stop=(z == PASSES - 1 and a == 1),
+                    start=(opens and a == 0),
+                    stop=(not opens and a == 1),
                 )
 
-        for u in range(len(units)):
-            for z in range(PASSES):
-                z_pass(u, z)
+        last = len(units) - 1
+        for u in range(last):
+            z_pass(u, 0, True)
+        for u in range(last):
+            z_pass(u, 1, False)
+        z_pass(last, 1, True)
+        z_pass(last, 0, False)
 
         xs_bf = [keep.tile([P, HALF, PACK], BF16, name="xs_bf%d" % h, align_bytes=64) for h in range(2)]
         xq = [keep.tile([P, HALF], U32, name="xq%d" % h, align_bytes=64) for h in range(2)]
@@ -132,58 +142,87 @@ def tile_list_peak_gated_members_kernel(tc, xt_words, xt_scales, w_words, w_scal
                     )
 
         W = 2 * HALF
-        peak = [keep.tile([P, W // GROUP], F32, name="peak%d" % u) for u in range(len(units))]
-        gap = [keep.tile([P, W], F32, name="gap%d" % u) for u in range(len(units))]
-        gate = [keep.tile([P, W], F32, name="gate%d" % u) for u in range(len(units))]
-        kept = [keep.tile([P, W], F32, name="kept%d" % u) for u in range(len(units))]
-        half_q = [keep.tile([P, W], F32, name="half_q%d" % u) for u in range(len(units) - 1)]
+        G = W // GROUP
+        peak2 = shared.tile([P, G], F32, name="peak2", align_bytes=64, offset=0)
+        late = shared.tile([P, 5 * W + G], F32, name="late", align_bytes=64, offset=6144)
+        free = keep.tile([P, 10 * W + 2 * G], F32, name="free")
+
+        def piece(tile, i, width=W, base=0):
+            return tile[:, base + i * width : base + (i + 1) * width]
+
+        peak = [piece(free, 0, G, 10 * W), piece(free, 1, G, 10 * W), peak2[:], piece(late, 0, G, 5 * W)]
+        gap = [piece(free, 0), piece(free, 1), piece(late, 0), piece(free, 2)]
+        gate = [piece(late, 1), piece(late, 2), piece(free, 3), piece(free, 4)]
+        kept = [piece(free, 5 + u) for u in range(len(units))]
+        half_q = [piece(late, 3), piece(late, 4), piece(free, 9)]
         res = [keep.tile([P, W], F32, name="res%d" % u) for u in range(len(units))]
         out_v = out.rearrange("(t p) j -> p t j", p=P)
 
         def find_peak(u):
-            nc.vector.tensor_reduce(out=peak[u][:], in_=zb[u][:].rearrange("p (g m) -> p g m", m=GROUP), axis=mybir.AxisListType.X, op=ALU.max)
+            nc.vector.tensor_reduce(out=peak[u], in_=zb[u][:].rearrange("p (g m) -> p g m", m=GROUP), axis=mybir.AxisListType.X, op=ALU.max)
 
-        def find_gate(u):
+        def find_gap(u):
             nc.vector.tensor_tensor(
-                out=gap[u][:].rearrange("p (g m) -> p g m", m=GROUP),
+                out=gap[u].rearrange("p (g m) -> p g m", m=GROUP),
                 in0=zb[u][:].rearrange("p (g m) -> p g m", m=GROUP),
-                in1=peak[u][:].unsqueeze(2).to_broadcast([P, W // GROUP, GROUP]),
+                in1=peak[u].unsqueeze(2).to_broadcast([P, W // GROUP, GROUP]),
                 op=ALU.subtract,
             )
-            nc.scalar.activation(out=gate[u][:], in_=gap[u][:], func=ACT.Exp)
+
+        def find_gate(u):
+            nc.scalar.activation(out=gate[u], in_=gap[u], func=ACT.Exp)
 
         def apply_gate(u):
-            nc.vector.tensor_tensor(out=kept[u][:], in0=zb[u][:], in1=gate[u][:], op=ALU.mult)
+            nc.vector.tensor_tensor(out=kept[u], in0=zb[u][:], in1=gate[u], op=ALU.mult)
 
-        def finish(u):
+        def halve_q(u, tiles):
+            cols = slice(tiles.start * HALF, tiles.stop * HALF)
+            nc.scalar.activation(out=half_q[u][:, cols], in_=qb[u][:, cols], func=ACT.Copy, scale=0.5)
+
+        def store(u, tiles):
             h, pair = units[u]
-            if u < len(units) - 1:
-                nc.scalar.activation(out=half_q[u][:], in_=qb[u][:], func=ACT.Copy, scale=0.5)
-                nc.gpsimd.tensor_tensor(out=res[u][:], in0=kept[u][:], in1=half_q[u][:], op=ALU.add)
-            else:
-                nc.vector.scalar_tensor_tensor(out=res[u][:], in0=qb[u][:], scalar=0.5, in1=kept[u][:], op0=ALU.mult, op1=ALU.add)
             nc.sync.dma_start(
-                out=out_v[:, 2 * pair : 2 * pair + 2, h * HALF : (h + 1) * HALF],
-                in_=res[u][:].rearrange("p (a c) -> p a c", a=2),
+                out=out_v[:, 2 * pair + tiles.start : 2 * pair + tiles.stop, h * HALF : (h + 1) * HALF],
+                in_=res[u][:].rearrange("p (a c) -> p a c", a=2)[:, tiles, :],
             )
 
+        def finish_on_gpsimd(u, tiles):
+            cols = slice(tiles.start * HALF, tiles.stop * HALF)
+            nc.gpsimd.tensor_tensor(out=res[u][:, cols], in0=kept[u][:, cols], in1=half_q[u][:, cols], op=ALU.add)
+            store(u, tiles)
+
+        def finish_on_vector(u, tiles):
+            cols = slice(tiles.start * HALF, tiles.stop * HALF)
+            nc.vector.scalar_tensor_tensor(out=res[u][:, cols], in0=qb[u][:, cols], scalar=0.5, in1=kept[u][:, cols], op0=ALU.mult, op1=ALU.add)
+            store(u, tiles)
+
+        both, first, second = slice(0, 2), slice(0, 1), slice(1, 2)
         round_xs(0)
+        round_xs(1)
         find_peak(0)
         find_peak(1)
+        find_gap(0)
         find_gate(0)
-        q_product(0)
+        find_gap(1)
         find_gate(1)
+        q_product(0)
         find_peak(2)
+        q_product(1)
+        find_peak(3)
         apply_gate(0)
-        finish(0)
-        round_xs(1)
+        halve_q(0, both)
+        finish_on_gpsimd(0, both)
+        halve_q(1, both)
+        find_gap(2)
         find_gate(2)
         apply_gate(1)
-        finish(1)
-        find_peak(3)
-        q_product(1)
+        finish_on_gpsimd(1, both)
+        halve_q(2, first)
+        find_gap(3)
         find_gate(3)
         apply_gate(2)
-        finish(2)
+        finish_on_gpsimd(2, first)
         apply_gate(3)
-        finish(3)
+        finish_on_vector(2, second)
+        finish_on_vector(3, first)
+        finish_on_vector(3, second)

from contextlib import ExitStack

import concourse.mybir as mybir

K, T, J, L, N = 1024, 2048, 512, 512, 512
FLOPS = 2 * N * J * (K + L)

F32 = mybir.dt.float32
BF16 = mybir.dt.bfloat16
I32 = mybir.dt.int32
U32 = mybir.dt.uint32
U16 = mybir.dt.uint16
U8 = mybir.dt.uint8
FP8X4 = mybir.dt.float8_e4m3fn_x4
FP4X4 = mybir.dt.float4_e2m1fn_x4
ALU = mybir.AluOpType
ACT = mybir.ActivationFunctionType

P = 128
PACK = 4
PASSES = K // (P * PACK)
GROUP = 4
HALF = J // 2
PAIRS = N // (2 * P)


def load_scale_rows(queue, plane, rows):
    passes = rows.shape[0]
    src = rows.bitcast(I32).rearrange("z (q r) c -> r q z c", r=4)
    dst = plane[:].bitcast(I32)
    for r in range(4):
        queue.dma_start(out=dst[r:P:32, :].rearrange("q (z c) -> q z c", z=passes), in_=src[r])


def tile_list_peak_gated_members_kernel(tc, xt_words, xt_scales, w_words, w_scales, xs, ws_words, ws_scales, offs, out):
    nc = tc.nc
    with ExitStack() as ctx:
        keep = ctx.enter_context(tc.tile_pool(name="keep", bufs=1))
        shared = ctx.enter_context(tc.tile_pool(name="shared", bufs=1))
        psum = ctx.enter_context(tc.psum_pool(name="psum", bufs=1))

        offsets = keep.tile([P, J // 16], U16, name="offsets")
        xt = [keep.tile([P, T], U32, name="xt%d" % z, tag="xt_slot%d" % z, align_bytes=64) for z in range(PASSES)]
        xt_sc = shared.tile([P, T], U8, name="xt_sc", align_bytes=64, offset=4032)
        w = keep.tile([P, PASSES, 2 * N], U8, name="w", align_bytes=64)
        w_sc = keep.tile([P, PASSES * N], U8, name="w_sc", align_bytes=64)
        ws = keep.tile([P, N], U32, name="ws", tag="xt_slot0", align_bytes=64)
        ws_sc = shared.tile([P, N], U8, name="ws_sc", align_bytes=64, offset=4096)
        xs_raw = [
            shared.tile([P, PACK, HALF], F32, name="xs_raw0", align_bytes=64, offset=0),
            shared.tile([P, PACK, HALF], F32, name="xs_raw1", align_bytes=64, offset=6016),
        ]
        moved_sc = keep.tile([P, J], U8, name="moved_sc", align_bytes=64)

        nc.vector.memset(xt_sc[:].bitcast(I32), 0)
        nc.gpsimd.memset(w_sc[:].bitcast(I32), 0)
        nc.gpsimd.memset(moved_sc[:].bitcast(I32), 0)

        def load_words(z, cols):
            nc.sync.dma_start(out=xt[z][:].bitcast(I32)[:, cols], in_=xt_words[z].rearrange("p c r -> p (c r)").bitcast(I32)[:, cols])

        def load_xs(h):
            nc.sync.dma_start(out=xs_raw[h][:], in_=xs.rearrange("(p i) j -> p i j", i=PACK)[:, :, h * HALF : (h + 1) * HALF])

        nc.sync.dma_start(offsets[:], offs)
        load_words(0, slice(0, T // 2))
        for r in range(4):
            nc.sync.dma_start(
                out=xt_sc[:].bitcast(I32)[r:P:16, :],
                in_=xt_scales.bitcast(I32).rearrange("z (q r) c -> r q z c", r=4)[r],
            )
        load_words(0, slice(T // 2, T))
        nc.sync.dma_start(out=w[:].bitcast(I32), in_=w_words.bitcast(I32).rearrange("z p c -> p z c"))
        load_scale_rows(nc.sync, w_sc, w_scales)
        load_words(1, slice(0, T))

        picked = [[keep.tile([P, HALF], U32, name="picked%d_%d" % (z, h), align_bytes=64) for h in range(2)] for z in range(PASSES)]
        both_sc = keep.tile([P, J], U8, name="both_sc", align_bytes=64)
        picked_sc = [both_sc, moved_sc]
        nc.vector.tensor_copy(both_sc[:], xt_sc[:].indirect(offsets[:]))
        nc.sync.dma_start(out=moved_sc[:].bitcast(I32)[0 : P - 16, :], in_=both_sc[:].bitcast(I32)[16:P, :])
        load_xs(0)
        load_xs(1)
        nc.gpsimd.memset(ws_sc[:].bitcast(I32), 0)
        load_scale_rows(nc.sync, ws_sc, ws_scales)
        for z in range(PASSES):
            for h in range(2):
                nc.vector.tensor_copy(picked[z][h][:], xt[z][:].indirect(offsets[:, h * HALF // 16 : (h + 1) * HALF // 16]))
        nc.sync.dma_start(out=ws[:].bitcast(I32), in_=ws_words[0].rearrange("p c r -> p (c r)").bitcast(I32))

        units = [(h, pair) for h in range(2) for pair in range(PAIRS)]
        zb = [psum.tile([P, 2 * HALF], F32, name="z%d" % u) for u in range(len(units))]
        qb = [psum.tile([P, 2 * HALF], F32, name="q%d" % u) for u in range(len(units))]

        def z_pass(u, z, opens):
            h, pair = units[u]
            cols = slice(h * HALF, (h + 1) * HALF)
            for a in range(2):
                t = 2 * pair + a
                nc.tensor.matmul_mx(
                    out=zb[u][:, a * HALF : (a + 1) * HALF],
                    lhsT=w[:, z, 2 * P * t : 2 * P * (t + 1)].bitcast(FP4X4),
                    lhsT_scale=w_sc[:, z * N + P * t : z * N + P * (t + 1)],
                    rhs=picked[z][h][:].bitcast(FP8X4),
                    rhs_scale=picked_sc[z][:, cols],
                    start=(opens and a == 0),
                    stop=(not opens and a == 1),
                )

        last = len(units) - 1
        for u in range(last):
            z_pass(u, 0, True)
        for u in range(last):
            z_pass(u, 1, False)
        z_pass(last, 1, True)
        z_pass(last, 0, False)

        xs_bf = [keep.tile([P, HALF, PACK], BF16, name="xs_bf%d" % h, align_bytes=64) for h in range(2)]
        xq = [keep.tile([P, HALF], U32, name="xq%d" % h, align_bytes=64) for h in range(2)]
        xq_sc = [keep.tile([P, HALF], U8, name="xq_sc%d" % h, align_bytes=64) for h in range(2)]

        def round_xs(h):
            nc.scalar.activation(
                out=xs_bf[h][:].rearrange("p (c i) t -> p c t i", i=4),
                in_=xs_raw[h][:].rearrange("p t (c i) -> p c t i", i=4),
                func=ACT.Copy,
            )

        def q_product(h):
            nc.vector.quantize_mx(out=xq[h][:].bitcast(FP8X4), scales=xq_sc[h][:], in_=xs_bf[h][:].rearrange("p c t -> p (c t)"))
            for pair in range(PAIRS):
                for a in range(2):
                    t = 2 * pair + a
                    nc.tensor.matmul_mx(
                        out=qb[h * PAIRS + pair][:, a * HALF : (a + 1) * HALF],
                        lhsT=ws[:, P * t : P * (t + 1)].bitcast(FP8X4),
                        lhsT_scale=ws_sc[:, P * t : P * (t + 1)],
                        rhs=xq[h][:].bitcast(FP8X4),
                        rhs_scale=xq_sc[h][:],
                        start=True,
                        stop=True,
                    )

        W = 2 * HALF
        G = W // GROUP
        peak2 = shared.tile([P, G], F32, name="peak2", align_bytes=64, offset=0)
        late = shared.tile([P, 5 * W + G], F32, name="late", align_bytes=64, offset=6144)
        free = keep.tile([P, 10 * W + 2 * G], F32, name="free")

        def piece(tile, i, width=W, base=0):
            return tile[:, base + i * width : base + (i + 1) * width]

        peak = [piece(free, 0, G, 10 * W), piece(free, 1, G, 10 * W), peak2[:], piece(late, 0, G, 5 * W)]
        gap = [piece(free, 0), piece(free, 1), piece(late, 0), piece(free, 2)]
        gate = [piece(late, 1), piece(late, 2), piece(free, 3), piece(free, 4)]
        kept = [piece(free, 5 + u) for u in range(len(units))]
        half_q = [piece(late, 3), piece(late, 4), piece(free, 9)]
        res = [keep.tile([P, W], F32, name="res%d" % u) for u in range(len(units))]
        out_v = out.rearrange("(t p) j -> p t j", p=P)

        def find_peak(u):
            nc.vector.tensor_reduce(out=peak[u], in_=zb[u][:].rearrange("p (g m) -> p g m", m=GROUP), axis=mybir.AxisListType.X, op=ALU.max)

        def find_gap(u):
            nc.vector.tensor_tensor(
                out=gap[u].rearrange("p (g m) -> p g m", m=GROUP),
                in0=zb[u][:].rearrange("p (g m) -> p g m", m=GROUP),
                in1=peak[u].unsqueeze(2).to_broadcast([P, W // GROUP, GROUP]),
                op=ALU.subtract,
            )

        def find_gate(u):
            nc.scalar.activation(out=gate[u], in_=gap[u], func=ACT.Exp)

        def apply_gate(u):
            nc.vector.tensor_tensor(out=kept[u], in0=zb[u][:], in1=gate[u], op=ALU.mult)

        def halve_q(u, tiles):
            cols = slice(tiles.start * HALF, tiles.stop * HALF)
            nc.scalar.activation(out=half_q[u][:, cols], in_=qb[u][:, cols], func=ACT.Copy, scale=0.5)

        def store(u, tiles):
            h, pair = units[u]
            nc.sync.dma_start(
                out=out_v[:, 2 * pair + tiles.start : 2 * pair + tiles.stop, h * HALF : (h + 1) * HALF],
                in_=res[u][:].rearrange("p (a c) -> p a c", a=2)[:, tiles, :],
            )

        def finish_on_gpsimd(u, tiles):
            cols = slice(tiles.start * HALF, tiles.stop * HALF)
            nc.gpsimd.tensor_tensor(out=res[u][:, cols], in0=kept[u][:, cols], in1=half_q[u][:, cols], op=ALU.add)
            store(u, tiles)

        def finish_on_vector(u, tiles):
            cols = slice(tiles.start * HALF, tiles.stop * HALF)
            nc.vector.scalar_tensor_tensor(out=res[u][:, cols], in0=qb[u][:, cols], scalar=0.5, in1=kept[u][:, cols], op0=ALU.mult, op1=ALU.add)
            store(u, tiles)

        both, first, second = slice(0, 2), slice(0, 1), slice(1, 2)
        round_xs(0)
        round_xs(1)
        find_peak(0)
        find_peak(1)
        find_gap(0)
        find_gate(0)
        find_gap(1)
        find_gate(1)
        q_product(0)
        find_peak(2)
        q_product(1)
        find_peak(3)
        apply_gate(0)
        halve_q(0, both)
        finish_on_gpsimd(0, both)
        halve_q(1, both)
        find_gap(2)
        find_gate(2)
        apply_gate(1)
        finish_on_gpsimd(1, both)
        halve_q(2, first)
        find_gap(3)
        find_gate(3)
        apply_gate(2)
        finish_on_gpsimd(2, first)
        apply_gate(3)
        finish_on_vector(2, second)
        finish_on_vector(3, first)
        finish_on_vector(3, second)
